import numpy as np, ml_dtypes
CORES = [83,85,87,115,117,119]
N = 6
import mx_ref
NC, ROOT = 128, 4
C = np.float32(0.029)
BF = ml_dtypes.bfloat16
def cut(t, i, w=512):
    return t[:, w * i:w * i + w]
def tile(rs):
    return np.stack(rs, axis=2).reshape(128, -1).astype(BF)
def pick(b):
    s = np.zeros((128, 128, 4), np.float32)
    s[np.arange(128), np.arange(128), b] = 1.0
    return mx_ref.quantize(s.reshape(128, 512).astype(BF))
def pk(c, s, i=0):
    return (np.ascontiguousarray(c[:, 512 * i:512 * i + 512]), mx_ref.live(s[:, 128 * i:128 * i + 128]))
def inputs(rng, e, E):
    def f(*shape):
        v = (rng.standard_normal(shape, dtype=np.float32) * np.exp2(rng.integers(-2, 3, shape[:-1] + (1,)))).astype(BF)
        return mx_ref.spread((v.astype(np.float32) * np.exp2(rng.integers(-E, E + 1, shape[:-2] + (1, 1))).astype(np.float32)).astype(BF), rng, e)
    def packed(k):
        c = np.zeros((N, 128, k * 512), np.uint8); s = np.zeros((N, 128, k * 128), np.uint8)
        for r in range(N):
            for i in range(k):
                a, b = mx_ref.quantize(f(128, 512)); c[r][:, 512 * i:512 * i + 512] = a; s[r][:, 128 * i:128 * i + 128] = mx_ref.plane(b, rng)
        return c, s
    d = {}
    d["wc"], d["ws"] = packed(1)
    d["a"] = f(N, 128, 512)
    d["bb"] = f(N, 128, 4 * 512)
    d["x"] = f(N, 128, 4 * NC)
    return d
def setup_inputs(rng):
    return inputs(rng, 0, 0)
def setup_inputs_blocks(rng):
    return inputs(rng, 2, 0)
def setup_inputs_wide(rng):
    return inputs(rng, 0, 3)
def reference(wc, ws, a, bb, x):
    S = [pick(t) for t in range(4)]; A = mx_ref.quantize(a[ROOT])
    V = [mx_ref.quantize(tile([mx_ref.matmul(S[t], pk(wc[j], ws[j])) + mx_ref.matmul(mx_ref.quantize(cut(bb[j], t)), A) * C for t in range(4)])) for j in range(N)]
    y = np.zeros((N, 128, N * NC), np.float32)
    for r in range(N):
        X = mx_ref.quantize(x[r])
        for j in range(N):
            y[r][:, NC * j:NC * j + NC] = mx_ref.matmul(V[j], X)
    return {"y": y}

@@ -1,0 +1,167 @@
+from concourse.bass import DstId, RemoteDMATransfer
+from concourse.mybir import dt, AluOpType, ActivationFunctionType
+
+N = 6
+NC = 128
+SCALE = 0.029
+
+SCRATCH = {
+    "a_t": ("sbuf", [128, 512], "bfloat16"),
+    "bb_t": ("sbuf", [128, 2048], "bfloat16"),
+    "x_t": ("sbuf", [128, 512], "bfloat16"),
+    "ones": ("sbuf", [128, 128], "bfloat16"),
+    "ident": ("sbuf", [128, 128], "bfloat16"),
+    "s_t": ("sbuf", [128, 2048], "bfloat16"),
+    "v_t": ("sbuf", [128, 512], "bfloat16"),
+    "m": ("sbuf", [128, 512], "float32"),
+    "yo": ("sbuf", [128, N * NC], "float32"),
+    "qa": ("sbuf", [128, 128], "float8_e4m3fn_x4"),
+    "pa": ("sbuf", [128, 128], "uint8"),
+    "qb": ("sbuf", [128, 512], "float8_e4m3fn_x4"),
+    "pb": ("sbuf", [128, 512], "uint8"),
+    "qs": ("sbuf", [128, 512], "float8_e4m3fn_x4"),
+    "ps": ("sbuf", [128, 512], "uint8"),
+    "qx": ("sbuf", [128, 128], "float8_e4m3fn_x4"),
+    "px": ("sbuf", [128, 128], "uint8"),
+    "qw": ("sbuf", [128, 128], "float8_e4m3fn_x4"),
+    "pw": ("sbuf", [128, 128], "uint8"),
+    "qv": ("sbuf", [128, N * 128], "float8_e4m3fn_x4"),
+    "pv": ("sbuf", [128, N * 128], "uint8"),
+    "d": ("psum", [128, 2048], "float32"),
+    "p": ("psum", [128, 2048], "float32"),
+}
+SEMAPHORES = (
+    ["ld_a", "ld_b", "ld_w", "ld_x", "ones_ok", "zero_ok", "id_ok", "s_ok", "a_ok", "qs_ok", "qb_ok", "qx_ok", "d_ok", "v_ok", "sent", "arr_a", "st"]
+    + ["prod%d" % b for b in range(4)] + ["mul%d" % b for b in range(4)] + ["add%d" % b for b in range(4)]
+    + ["arr%d" % j for j in range(N)] + ["y%d" % j for j in range(N)] + ["c%d" % j for j in range(N)]
+)
+
+
+def bits(mask):
+    return bin(mask).count("1")
+
+
+def cut(b, w):
+    return slice(w * b, w * b + w)
+
+
+def rank_program(g, core, T, topo):
+    rank = T.rank_of(core)
+    if rank is None:
+        return
+    sem = T.sem
+    root = T.root
+    copy = ActivationFunctionType.Copy
+    others = [c for c in T.cores if c != core]
+    far = sorted([c for c in others if topo.chip(c) != topo.chip(core)], key=lambda c: (topo.die(c) != topo.die(core), c))
+    near = [c for c in others if topo.chip(c) == topo.chip(core)]
+
+    def masks(src):
+        f = [topo.mask(src, c) for c in T.cores if topo.chip(c) != topo.chip(src)][0]
+        n = [topo.mask(src, c) for c in T.cores if c != src and topo.chip(c) == topo.chip(src)][0]
+        return f, n & ~f
+
+    def raised(src, dst):
+        f, n = masks(src)
+        return bits(f if topo.chip(src) != topo.chip(dst) else n)
+
+    sent = [0]
+
+    def put(view, dsts, mask, arrived):
+        ids = []
+        for c in dsts:
+            rid, pid, _ = topo.addr(c)
+            ids.append(DstId(rid=rid, pnc=pid))
+        g.remote_dma_fused([RemoteDMATransfer(dst_ids=ids, dma_engine_mask=mask, remote_sem=arrived,
+                                              srcs=[view], dsts=[view for _ in dsts])], local_sem=sem.sent)
+        sent[0] += bits(mask)
+
+    def spread(codes, plane, arrived):
+        f, n = masks(core)
+        for dsts, mask in ((far, f), (near, n)):
+            put(codes, dsts, mask, arrived)
+            put(plane, dsts, mask, arrived)
+
+    w_queue = g.scalar
+    if rank == root:
+        w_queue = g.sync
+        g.sync.dma_start(T.a_t[:], T.a[:]).then_inc(sem.ld_a, 16)
+    g.sync.dma_start(T.bb_t[:], T.bb[:]).then_inc(sem.ld_b, 16)
+    w_queue.dma_start(T.qw[:].bitcast(dt.uint8), T.wc[:]).then_inc(sem.ld_w, 16)
+    w_queue.dma_start(T.pw[:], T.ws[:]).then_inc(sem.ld_w, 16)
+    w_queue.dma_start(T.x_t[:], T.x[:]).then_inc(sem.ld_x, 16)
+
+    g.vector.memset(T.ones[:], 1.0).then_inc(sem.ones_ok, 1)
+    g.vector.memset(T.s_t[:], 0.0).then_inc(sem.zero_ok, 1)
+    g.wait_ge(sem.ones_ok, 1)
+    g.affine_select(T.ident[:], T.ones[:], [[-1, 128]], AluOpType.is_equal, 0.0, 0, 1).then_inc(sem.id_ok, 1)
+    g.scalar.wait_ge(sem.zero_ok, 1)
+    g.scalar.wait_ge(sem.id_ok, 1)
+    for b in range(4):
+        g.scalar.activation(T.s_t[:, 512 * b + b:512 * b + 512:4], T.ident[:], copy).then_inc(sem.s_ok, 1)
+
+    if rank == root:
+        g.vector.wait_ge(sem.ld_a, 16)
+        g.vector.quantize_mx(T.qa[:], T.pa[:], T.a_t[:]).then_inc(sem.a_ok, 1)
+    g.vector.wait_ge(sem.s_ok, 4)
+    g.vector.quantize_mx(T.qs[:], T.ps[:], T.s_t[:]).then_inc(sem.qs_ok, 1)
+    g.vector.wait_ge(sem.ld_b, 16)
+    g.vector.quantize_mx(T.qb[:], T.pb[:], T.bb_t[:]).then_inc(sem.qb_ok, 1)
+    g.vector.wait_ge(sem.ld_x, 16)
+    g.vector.quantize_mx(T.qx[:], T.px[:], T.x_t[:]).then_inc(sem.qx_ok, 1)
+
+    if rank == root:
+        g.wait_ge(sem.a_ok, 1)
+        spread(T.qa[:].bitcast(dt.uint8), T.pa[:], sem.arr_a)
+
+    te = g.tensor
+    te.wait_ge(sem.qs_ok, 1)
+    te.wait_ge(sem.ld_w, 32)
+    for b in range(4):
+        te.matmul_mx(T.d[:, 512 * b:512 * b + 128], T.qs[:, cut(b, 128)], T.ps[:, cut(b, 128)],
+                     T.qw[:], T.pw[:], True, True).then_inc(sem.d_ok, 1)
+    te.wait_ge(sem.qb_ok, 1)
+    if rank == root:
+        te.wait_ge(sem.a_ok, 1)
+    else:
+        te.wait_ge(sem.arr_a, 2 * raised(T.cores[root], core))
+    for b in range(4):
+        te.matmul_mx(T.p[:, 512 * b:512 * b + 128], T.qb[:, cut(b, 128)], T.pb[:, cut(b, 128)],
+                     T.qa[:], T.pa[:], True, True).then_inc(sem["prod%d" % b], 1)
+
+    g.vector.wait_ge(sem.d_ok, 4)
+    for b in range(4):
+        g.scalar.wait_ge(sem["prod%d" % b], 1)
+        g.scalar.activation(T.m[:, cut(b, 128)], T.p[:, 512 * b:512 * b + 128], copy, scale=SCALE).then_inc(sem["mul%d" % b], 1)
+        g.vector.wait_ge(sem["mul%d" % b], 1)
+        g.vector.tensor_tensor(T.v_t[:, b:512:4], T.m[:, cut(b, 128)], T.d[:, 512 * b:512 * b + 128],
+                               AluOpType.add).then_inc(sem["add%d" % b], 1)
+    for b in range(4):
+        g.vector.wait_ge(sem["add%d" % b], 1)
+    mine = cut(rank, 128)
+    g.vector.quantize_mx(T.qv[:, mine], T.pv[:, mine], T.v_t[:]).then_inc(sem.v_ok, 1)
+
+    g.wait_ge(sem.v_ok, 1)
+    spread(T.qv[:, mine].bitcast(dt.uint8), T.pv[:, mine], sem["arr%d" % rank])
+
+    order = [rank]
+    for group in (near, far):
+        order += sorted([T.rank_of(c) for c in group], key=lambda j: (j != root, topo.die(T.cores[j]), j))
+    te.wait_ge(sem.qx_ok, 1)
+    te.wait_ge(sem.v_ok, 1)
+    for k, j in enumerate(order):
+        bank = T.p[:, 512 * k:512 * k + 128] if k < 4 else T.d[:, 512 * (k - 4):512 * (k - 4) + 128]
+        if j != rank:
+            te.wait_ge(sem["arr%d" % j], 2 * raised(T.cores[j], core))
+        te.matmul_mx(bank, T.qv[:, cut(j, 128)], T.pv[:, cut(j, 128)], T.qx[:], T.px[:], True, True).then_inc(sem["y%d" % j], 1)
+        out = T.yo[:, cut(j, NC)]
+        if k % 2:
+            g.vector.wait_ge(sem["y%d" % j], 1)
+            g.vector.tensor_copy(out, bank).then_inc(sem["c%d" % j], 1)
+        else:
+            g.scalar.wait_ge(sem["y%d" % j], 1)
+            g.scalar.activation(out, bank, copy).then_inc(sem["c%d" % j], 1)
+        g.sync.wait_ge(sem["c%d" % j], 1)
+        g.sync.dma_start(T.y[:, cut(j, NC)], out).then_inc(sem.st, 16)
+    g.sync.wait_ge(sem.st, 16 * N)
+    g.wait_ge(sem.sent, sent[0])

@@ -31,9 +31,9 @@ SCRATCH = {
     "p": ("psum", [128, 2048], "float32"),
 }
 SEMAPHORES = (
-    ["ld_a", "ld_b", "ld_w", "ld_x", "ones_ok", "zero_ok", "id_ok", "s_ok", "a_ok", "qs_ok", "qb_ok", "qx_ok", "d_ok", "v_ok", "sent", "arr_a", "st"]
+    ["ld_a", "ld_b", "ld_w", "ld_x", "ones_ok", "zero_ok", "id_ok", "s_ok", "a_ok", "qs_ok", "qb_ok", "qx_ok", "d_ok", "v_ok", "sent", "st", "ca", "sa"]
     + ["prod%d" % b for b in range(4)] + ["mul%d" % b for b in range(4)] + ["add%d" % b for b in range(4)]
-    + ["arr%d" % j for j in range(N)] + ["y%d" % j for j in range(N)] + ["c%d" % j for j in range(N)]
+    + ["%s%d" % (s, j) for s in ("cv", "sv", "y", "o") for j in range(N)]
 )
 
 
@@ -45,6 +45,21 @@ def cut(b, w):
     return slice(w * b, w * b + w)
 
 
+def hops(T, topo, j, is_a):
+    src = T.cores[j]
+    here = [c for c in T.cores if topo.chip(c) == topo.chip(src)]
+    there = [c for c in T.cores if topo.chip(c) != topo.chip(src)]
+    near = [c for c in here if c != src]
+    first = sorted(there, key=lambda c: (topo.die(c) != topo.die(src), c)) if is_a else [there[here.index(src)]]
+    rest = [c for c in there if c not in first]
+    far_engines = topo.mask(src, first[0])
+    near_engines = topo.mask(src, near[0])
+    road = [(src, first, far_engines), (src, near, near_engines & ~far_engines)]
+    if rest:
+        road.append((first[0], rest, topo.mask(first[0], rest[0])))
+    return road
+
+
 def rank_program(g, core, T, topo):
     rank = T.rank_of(core)
     if rank is None:
@@ -52,19 +67,6 @@ def rank_program(g, core, T, topo):
     sem = T.sem
     root = T.root
     copy = ActivationFunctionType.Copy
-    others = [c for c in T.cores if c != core]
-    far = sorted([c for c in others if topo.chip(c) != topo.chip(core)], key=lambda c: (topo.die(c) != topo.die(core), c))
-    near = [c for c in others if topo.chip(c) == topo.chip(core)]
-
-    def masks(src):
-        f = [topo.mask(src, c) for c in T.cores if topo.chip(c) != topo.chip(src)][0]
-        n = [topo.mask(src, c) for c in T.cores if c != src and topo.chip(c) == topo.chip(src)][0]
-        return f, n & ~f
-
-    def raised(src, dst):
-        f, n = masks(src)
-        return bits(f if topo.chip(src) != topo.chip(dst) else n)
-
     sent = [0]
 
     def put(view, dsts, mask, arrived):
@@ -76,11 +78,22 @@ def rank_program(g, core, T, topo):
                                               srcs=[view], dsts=[view for _ in dsts])], local_sem=sem.sent)
         sent[0] += bits(mask)
 
-    def spread(codes, plane, arrived):
-        f, n = masks(core)
-        for dsts, mask in ((far, f), (near, n)):
-            put(codes, dsts, mask, arrived)
-            put(plane, dsts, mask, arrived)
+    def landed(j, is_a):
+        for s, dsts, mask in hops(T, topo, j, is_a):
+            if core in dsts:
+                return bits(mask)
+
+    def spread(j, is_a):
+        codes, plane = (T.qa[:], T.pa[:]) if is_a else (T.qv[:, cut(j, 128)], T.pv[:, cut(j, 128)])
+        c_sem, s_sem = (sem.ca, sem.sa) if is_a else (sem["cv%d" % j], sem["sv%d" % j])
+        for s, dsts, mask in hops(T, topo, j, is_a):
+            if s == core:
+                if j != rank:
+                    g.wait_ge(c_sem, landed(j, is_a))
+                put(codes.bitcast(dt.uint8), dsts, mask, c_sem)
+                if j != rank:
+                    g.wait_ge(s_sem, landed(j, is_a))
+                put(plane, dsts, mask, s_sem)
 
     w_queue = g.scalar
     if rank == root:
@@ -112,7 +125,7 @@ def rank_program(g, core, T, topo):
 
     if rank == root:
         g.wait_ge(sem.a_ok, 1)
-        spread(T.qa[:].bitcast(dt.uint8), T.pa[:], sem.arr_a)
+        spread(root, True)
 
     te = g.tensor
     te.wait_ge(sem.qs_ok, 1)
@@ -124,7 +137,8 @@ def rank_program(g, core, T, topo):
     if rank == root:
         te.wait_ge(sem.a_ok, 1)
     else:
-        te.wait_ge(sem.arr_a, 2 * raised(T.cores[root], core))
+        te.wait_ge(sem.ca, landed(root, True))
+        te.wait_ge(sem.sa, landed(root, True))
     for b in range(4):
         te.matmul_mx(T.p[:, 512 * b:512 * b + 128], T.qb[:, cut(b, 128)], T.pb[:, cut(b, 128)],
                      T.qa[:], T.pa[:], True, True).then_inc(sem["prod%d" % b], 1)
@@ -142,26 +156,31 @@ def rank_program(g, core, T, topo):
     g.vector.quantize_mx(T.qv[:, mine], T.pv[:, mine], T.v_t[:]).then_inc(sem.v_ok, 1)
 
     g.wait_ge(sem.v_ok, 1)
-    spread(T.qv[:, mine].bitcast(dt.uint8), T.pv[:, mine], sem["arr%d" % rank])
+    spread(rank, False)
+    for j in range(N):
+        if j != rank:
+            spread(j, False)
 
-    order = [rank]
-    for group in (near, far):
-        order += sorted([T.rank_of(c) for c in group], key=lambda j: (j != root, topo.die(T.cores[j]), j))
+    def place(j):
+        c = T.cores[j]
+        return (j != rank, topo.chip(c) != topo.chip(core), core not in hops(T, topo, j, False)[0][1], j != root, j)
+
     te.wait_ge(sem.qx_ok, 1)
     te.wait_ge(sem.v_ok, 1)
-    for k, j in enumerate(order):
+    for k, j in enumerate(sorted(range(N), key=place)):
         bank = T.p[:, 512 * k:512 * k + 128] if k < 4 else T.d[:, 512 * (k - 4):512 * (k - 4) + 128]
         if j != rank:
-            te.wait_ge(sem["arr%d" % j], 2 * raised(T.cores[j], core))
+            te.wait_ge(sem["cv%d" % j], landed(j, False))
+            te.wait_ge(sem["sv%d" % j], landed(j, False))
         te.matmul_mx(bank, T.qv[:, cut(j, 128)], T.pv[:, cut(j, 128)], T.qx[:], T.px[:], True, True).then_inc(sem["y%d" % j], 1)
         out = T.yo[:, cut(j, NC)]
         if k % 2:
             g.vector.wait_ge(sem["y%d" % j], 1)
-            g.vector.tensor_copy(out, bank).then_inc(sem["c%d" % j], 1)
+            g.vector.tensor_copy(out, bank).then_inc(sem["o%d" % j], 1)
         else:
             g.scalar.wait_ge(sem["y%d" % j], 1)
-            g.scalar.activation(out, bank, copy).then_inc(sem["c%d" % j], 1)
-        g.sync.wait_ge(sem["c%d" % j], 1)
+            g.scalar.activation(out, bank, copy).then_inc(sem["o%d" % j], 1)
+        g.sync.wait_ge(sem["o%d" % j], 1)
         g.sync.dma_start(T.y[:, cut(j, NC)], out).then_inc(sem.st, 16)
     g.sync.wait_ge(sem.st, 16 * N)
     g.wait_ge(sem.sent, sent[0])

@@ -9,9 +9,7 @@ SCRATCH = {
     "a_t": ("sbuf", [128, 512], "bfloat16"),
     "bb_t": ("sbuf", [128, 2048], "bfloat16"),
     "x_t": ("sbuf", [128, 512], "bfloat16"),
-    "ones": ("sbuf", [128, 128], "bfloat16"),
-    "ident": ("sbuf", [128, 128], "bfloat16"),
-    "s_t": ("sbuf", [128, 2048], "bfloat16"),
+    "s_t": ("sbuf", [128, 1536], "bfloat16"),
     "v_t": ("sbuf", [128, 512], "bfloat16"),
     "m": ("sbuf", [128, 512], "float32"),
     "yo": ("sbuf", [128, N * NC], "float32"),
@@ -31,7 +29,8 @@ SCRATCH = {
     "p": ("psum", [128, 2048], "float32"),
 }
 SEMAPHORES = (
-    ["ld_a", "ld_b", "ld_w", "ld_x", "ones_ok", "zero_ok", "id_ok", "s_ok", "a_ok", "qs_ok", "qb_ok", "qx_ok", "d_ok", "v_ok", "sent", "st", "ca", "sa"]
+    ["ld_a", "ld_b", "ld_w", "ld_x", "z1_ok", "z2_ok", "id_ok", "s_ok", "a_ok", "qs_ok", "qb_ok", "qx_ok", "d_ok", "v_ok",
+     "sent", "st", "ca", "sa", "cs", "ss"]
     + ["prod%d" % b for b in range(4)] + ["mul%d" % b for b in range(4)] + ["add%d" % b for b in range(4)]
     + ["%s%d" % (s, j) for s in ("cv", "sv", "y", "o") for j in range(N)]
 )
@@ -69,13 +68,14 @@ def rank_program(g, core, T, topo):
     copy = ActivationFunctionType.Copy
     sent = [0]
 
-    def put(view, dsts, mask, arrived):
+    def put(view, dsts, mask, arrived, into=None):
         ids = []
         for c in dsts:
             rid, pid, _ = topo.addr(c)
             ids.append(DstId(rid=rid, pnc=pid))
+        target = view if into is None else into
         g.remote_dma_fused([RemoteDMATransfer(dst_ids=ids, dma_engine_mask=mask, remote_sem=arrived,
-                                              srcs=[view], dsts=[view for _ in dsts])], local_sem=sem.sent)
+                                              srcs=[view], dsts=[target for _ in dsts])], local_sem=sem.sent)
         sent[0] += bits(mask)
 
     def landed(j, is_a):
@@ -104,34 +104,51 @@ def rank_program(g, core, T, topo):
     w_queue.dma_start(T.pw[:], T.ws[:]).then_inc(sem.ld_w, 16)
     w_queue.dma_start(T.x_t[:], T.x[:]).then_inc(sem.ld_x, 16)
 
-    g.vector.memset(T.ones[:], 1.0).then_inc(sem.ones_ok, 1)
-    g.vector.memset(T.s_t[:], 0.0).then_inc(sem.zero_ok, 1)
-    g.wait_ge(sem.ones_ok, 1)
-    g.affine_select(T.ident[:], T.ones[:], [[-1, 128]], AluOpType.is_equal, 0.0, 0, 1).then_inc(sem.id_ok, 1)
-    g.scalar.wait_ge(sem.zero_ok, 1)
-    g.scalar.wait_ge(sem.id_ok, 1)
-    for b in range(4):
-        g.scalar.activation(T.s_t[:, 512 * b + b:512 * b + 512:4], T.ident[:], copy).then_inc(sem.s_ok, 1)
+    here = [c for c in T.cores if topo.chip(c) == topo.chip(core)]
+    place_here = here.index(core)
+    before, after = here[place_here - 1], here[(place_here + 1) % len(here)]
+    first, got = place_here, here.index(before)
+    slots = [first, got] + [b for b in range(4) if b not in (first, got)]
 
+    g.vector.memset(T.s_t[:, 0:512], 0.0).then_inc(sem.z1_ok, 1)
+    g.vector.memset(T.s_t[:, 512:1536], 0.0).then_inc(sem.z2_ok, 1)
+    ident = T.s_t[:, first:512:4]
+    g.wait_ge(sem.z1_ok, 1)
+    g.affine_select(ident, ident, [[-1, 128]], AluOpType.not_equal, 1.0, 0, 1).then_inc(sem.id_ok, 1)
+    g.scalar.wait_ge(sem.z2_ok, 1)
+    g.scalar.wait_ge(sem.id_ok, 1)
+    for i in (1, 2):
+        g.scalar.activation(T.s_t[:, 512 * i + slots[i + 1]:512 * i + 512:4], ident, copy).then_inc(sem.s_ok, 1)
+
+    g.vector.wait_ge(sem.id_ok, 1)
+    g.vector.quantize_mx(T.qs[:, 0:128], T.ps[:, 0:128], T.s_t[:, 0:512]).then_inc(sem.qs_ok, 1)
     if rank == root:
         g.vector.wait_ge(sem.ld_a, 16)
         g.vector.quantize_mx(T.qa[:], T.pa[:], T.a_t[:]).then_inc(sem.a_ok, 1)
-    g.vector.wait_ge(sem.s_ok, 4)
-    g.vector.quantize_mx(T.qs[:], T.ps[:], T.s_t[:]).then_inc(sem.qs_ok, 1)
+    g.vector.wait_ge(sem.s_ok, 2)
+    g.vector.quantize_mx(T.qs[:, 256:512], T.ps[:, 256:512], T.s_t[:, 512:1536]).then_inc(sem.qs_ok, 1)
     g.vector.wait_ge(sem.ld_b, 16)
     g.vector.quantize_mx(T.qb[:], T.pb[:], T.bb_t[:]).then_inc(sem.qb_ok, 1)
     g.vector.wait_ge(sem.ld_x, 16)
     g.vector.quantize_mx(T.qx[:], T.px[:], T.x_t[:]).then_inc(sem.qx_ok, 1)
+
+    pass_mask = topo.mask(core, after)
+    g.wait_ge(sem.qs_ok, 1)
+    put(T.qs[:, 0:128].bitcast(dt.uint8), [after], pass_mask, sem.cs, T.qs[:, 128:256].bitcast(dt.uint8))
+    put(T.ps[:, 0:128], [after], pass_mask, sem.ss, T.ps[:, 128:256])
 
     if rank == root:
         g.wait_ge(sem.a_ok, 1)
         spread(root, True)
 
     te = g.tensor
-    te.wait_ge(sem.qs_ok, 1)
+    te.wait_ge(sem.qs_ok, 2)
     te.wait_ge(sem.ld_w, 32)
-    for b in range(4):
-        te.matmul_mx(T.d[:, 512 * b:512 * b + 128], T.qs[:, cut(b, 128)], T.ps[:, cut(b, 128)],
+    for i in (0, 2, 3, 1):
+        if i == 1:
+            te.wait_ge(sem.cs, bits(topo.mask(before, core)))
+            te.wait_ge(sem.ss, bits(topo.mask(before, core)))
+        te.matmul_mx(T.d[:, 512 * slots[i]:512 * slots[i] + 128], T.qs[:, cut(i, 128)], T.ps[:, cut(i, 128)],
                      T.qw[:], T.pw[:], True, True).then_inc(sem.d_ok, 1)
     te.wait_ge(sem.qb_ok, 1)
     if rank == root:

@@ -44,19 +44,24 @@ def cut(b, w):
     return slice(w * b, w * b + w)
 
 
-def hops(T, topo, j, is_a):
+def legs(T, topo, j, is_a):
     src = T.cores[j]
     here = [c for c in T.cores if topo.chip(c) == topo.chip(src)]
     there = [c for c in T.cores if topo.chip(c) != topo.chip(src)]
     near = [c for c in here if c != src]
-    first = sorted(there, key=lambda c: (topo.die(c) != topo.die(src), c)) if is_a else [there[here.index(src)]]
-    rest = [c for c in there if c not in first]
-    far_engines = topo.mask(src, first[0])
-    near_engines = topo.mask(src, near[0])
-    road = [(src, first, far_engines), (src, near, near_engines & ~far_engines)]
-    if rest:
-        road.append((first[0], rest, topo.mask(first[0], rest[0])))
-    return road
+    far_engines = topo.mask(src, there[0])
+    near_engines = topo.mask(src, near[0]) & ~far_engines
+    if is_a:
+        crowd = sorted(there, key=lambda c: (-sum(topo.die(o) == topo.die(c) for o in there), c))
+        near = sorted(near, key=lambda c: (topo.die(c) != topo.die(src), c))
+        p, r, q = crowd
+        return [(src, [([p], far_engines), (near[:1], near_engines)]),
+                (src, [([q], far_engines), (near[1:], near_engines)]),
+                (p, [([r], topo.mask(p, r))])]
+    first = there[here.index(src)]
+    rest = [c for c in there if c != first]
+    return [(src, [([first], far_engines), (near, near_engines)]),
+            (first, [(rest, topo.mask(first, rest[0]))])]
 
 
 def rank_program(g, core, T, topo):
@@ -68,32 +73,39 @@ def rank_program(g, core, T, topo):
     copy = ActivationFunctionType.Copy
     sent = [0]
 
-    def put(view, dsts, mask, arrived, into=None):
-        ids = []
-        for c in dsts:
-            rid, pid, _ = topo.addr(c)
-            ids.append(DstId(rid=rid, pnc=pid))
+    def put(view, transfers, arrived, into=None):
         target = view if into is None else into
-        g.remote_dma_fused([RemoteDMATransfer(dst_ids=ids, dma_engine_mask=mask, remote_sem=arrived,
-                                              srcs=[view], dsts=[target for _ in dsts])], local_sem=sem.sent)
-        sent[0] += bits(mask)
+        batch = []
+        for dsts, mask in transfers:
+            ids = []
+            for c in dsts:
+                rid, pid, _ = topo.addr(c)
+                ids.append(DstId(rid=rid, pnc=pid))
+            batch.append(RemoteDMATransfer(dst_ids=ids, dma_engine_mask=mask, remote_sem=arrived,
+                                           srcs=[view], dsts=[target for _ in dsts]))
+            sent[0] += bits(mask)
+        g.remote_dma_fused(batch, local_sem=sem.sent)
+
+    def leg_to(j, is_a):
+        for n, (s, transfers) in enumerate(legs(T, topo, j, is_a)):
+            for dsts, mask in transfers:
+                if core in dsts:
+                    return n, bits(mask)
 
     def landed(j, is_a):
-        for s, dsts, mask in hops(T, topo, j, is_a):
-            if core in dsts:
-                return bits(mask)
+        return leg_to(j, is_a)[1]
 
     def spread(j, is_a):
         codes, plane = (T.qa[:], T.pa[:]) if is_a else (T.qv[:, cut(j, 128)], T.pv[:, cut(j, 128)])
         c_sem, s_sem = (sem.ca, sem.sa) if is_a else (sem["cv%d" % j], sem["sv%d" % j])
-        for s, dsts, mask in hops(T, topo, j, is_a):
+        for s, transfers in legs(T, topo, j, is_a):
             if s == core:
                 if j != rank:
                     g.wait_ge(c_sem, landed(j, is_a))
-                put(codes.bitcast(dt.uint8), dsts, mask, c_sem)
+                put(codes.bitcast(dt.uint8), transfers, c_sem)
                 if j != rank:
                     g.wait_ge(s_sem, landed(j, is_a))
-                put(plane, dsts, mask, s_sem)
+                put(plane, transfers, s_sem)
 
     w_queue = g.scalar
     if rank == root:
@@ -132,14 +144,14 @@ def rank_program(g, core, T, topo):
     g.vector.wait_ge(sem.ld_x, 16)
     g.vector.quantize_mx(T.qx[:], T.px[:], T.x_t[:]).then_inc(sem.qx_ok, 1)
 
-    pass_mask = topo.mask(core, after)
+    pass_on = [([after], topo.mask(core, after))]
     g.wait_ge(sem.qs_ok, 1)
-    put(T.qs[:, 0:128].bitcast(dt.uint8), [after], pass_mask, sem.cs, T.qs[:, 128:256].bitcast(dt.uint8))
-    put(T.ps[:, 0:128], [after], pass_mask, sem.ss, T.ps[:, 128:256])
+    put(T.qs[:, 0:128].bitcast(dt.uint8), pass_on, sem.cs, T.qs[:, 128:256].bitcast(dt.uint8))
+    put(T.ps[:, 0:128], pass_on, sem.ss, T.ps[:, 128:256])
 
     if rank == root:
         g.wait_ge(sem.a_ok, 1)
-        spread(root, True)
+    spread(root, True)
 
     te = g.tensor
     te.wait_ge(sem.qs_ok, 2)
@@ -162,10 +174,15 @@ def rank_program(g, core, T, topo):
 
     g.vector.wait_ge(sem.d_ok, 4)
     for b in range(4):
-        g.scalar.wait_ge(sem["prod%d" % b], 1)
-        g.scalar.activation(T.m[:, cut(b, 128)], T.p[:, 512 * b:512 * b + 128], copy, scale=SCALE).then_inc(sem["mul%d" % b], 1)
+        scaled, product = T.m[:, cut(b, 128)], T.p[:, 512 * b:512 * b + 128]
+        if b == 0:
+            g.vector.wait_ge(sem["prod%d" % b], 1)
+            g.vector.tensor_scalar(scaled, product, SCALE, None, AluOpType.mult).then_inc(sem["mul%d" % b], 1)
+        else:
+            g.scalar.wait_ge(sem["prod%d" % b], 1)
+            g.scalar.activation(scaled, product, copy, scale=SCALE).then_inc(sem["mul%d" % b], 1)
         g.vector.wait_ge(sem["mul%d" % b], 1)
-        g.vector.tensor_tensor(T.v_t[:, b:512:4], T.m[:, cut(b, 128)], T.d[:, 512 * b:512 * b + 128],
+        g.vector.tensor_tensor(T.v_t[:, b:512:4], scaled, T.d[:, 512 * b:512 * b + 128],
                                AluOpType.add).then_inc(sem["add%d" % b], 1)
     for b in range(4):
         g.vector.wait_ge(sem["add%d" % b], 1)
@@ -178,9 +195,14 @@ def rank_program(g, core, T, topo):
         if j != rank:
             spread(j, False)
 
+    turns = {root: 0}
+    for c in T.cores:
+        for n, (s, transfers) in enumerate(legs(T, topo, root, True)):
+            if any(c in dsts for dsts, mask in transfers):
+                turns[T.rank_of(c)] = 1 if n == 0 else 2
+
     def place(j):
-        c = T.cores[j]
-        return (j != rank, topo.chip(c) != topo.chip(core), core not in hops(T, topo, j, False)[0][1], j != root, j)
+        return (j != rank, j != rank and turns[j] + 2 * leg_to(j, False)[0], j)
 
     te.wait_ge(sem.qx_ok, 1)
     te.wait_ge(sem.v_ok, 1)

from concourse.bass import DstId, RemoteDMATransfer
from concourse.mybir import dt, AluOpType, ActivationFunctionType

N = 6
NC = 128
SCALE = 0.029

SCRATCH = {
    "a_t": ("sbuf", [128, 512], "bfloat16"),
    "bb_t": ("sbuf", [128, 2048], "bfloat16"),
    "x_t": ("sbuf", [128, 512], "bfloat16"),
    "s_t": ("sbuf", [128, 1536], "bfloat16"),
    "v_t": ("sbuf", [128, 512], "bfloat16"),
    "m": ("sbuf", [128, 512], "float32"),
    "yo": ("sbuf", [128, N * NC], "float32"),
    "qa": ("sbuf", [128, 128], "float8_e4m3fn_x4"),
    "pa": ("sbuf", [128, 128], "uint8"),
    "qb": ("sbuf", [128, 512], "float8_e4m3fn_x4"),
    "pb": ("sbuf", [128, 512], "uint8"),
    "qs": ("sbuf", [128, 512], "float8_e4m3fn_x4"),
    "ps": ("sbuf", [128, 512], "uint8"),
    "qx": ("sbuf", [128, 128], "float8_e4m3fn_x4"),
    "px": ("sbuf", [128, 128], "uint8"),
    "qw": ("sbuf", [128, 128], "float8_e4m3fn_x4"),
    "pw": ("sbuf", [128, 128], "uint8"),
    "qv": ("sbuf", [128, N * 128], "float8_e4m3fn_x4"),
    "pv": ("sbuf", [128, N * 128], "uint8"),
    "d": ("psum", [128, 2048], "float32"),
    "p": ("psum", [128, 2048], "float32"),
}
SEMAPHORES = (
    ["ld_a", "ld_b", "ld_w", "ld_x", "z1_ok", "z2_ok", "id_ok", "s_ok", "a_ok", "qs_ok", "qb_ok", "qx_ok", "d_ok", "v_ok",
     "sent", "st", "ca", "sa", "cs", "ss"]
    + ["prod%d" % b for b in range(4)] + ["mul%d" % b for b in range(4)] + ["add%d" % b for b in range(4)]
    + ["%s%d" % (s, j) for s in ("cv", "sv", "y", "o") for j in range(N)]
)


def bits(mask):
    return bin(mask).count("1")


def cut(b, w):
    return slice(w * b, w * b + w)


def legs(T, topo, j, is_a):
    src = T.cores[j]
    here = [c for c in T.cores if topo.chip(c) == topo.chip(src)]
    there = [c for c in T.cores if topo.chip(c) != topo.chip(src)]
    near = [c for c in here if c != src]
    far_engines = topo.mask(src, there[0])
    near_engines = topo.mask(src, near[0]) & ~far_engines
    if is_a:
        crowd = sorted(there, key=lambda c: (-sum(topo.die(o) == topo.die(c) for o in there), c))
        near = sorted(near, key=lambda c: (topo.die(c) != topo.die(src), c))
        p, r, q = crowd
        return [(src, [([p], far_engines), (near[:1], near_engines)]),
                (src, [([q], far_engines), (near[1:], near_engines)]),
                (p, [([r], topo.mask(p, r))])]
    first = there[here.index(src)]
    rest = [c for c in there if c != first]
    return [(src, [([first], far_engines), (near, near_engines)]),
            (first, [(rest, topo.mask(first, rest[0]))])]


def rank_program(g, core, T, topo):
    rank = T.rank_of(core)
    if rank is None:
        return
    sem = T.sem
    root = T.root
    copy = ActivationFunctionType.Copy
    sent = [0]

    def put(view, transfers, arrived, into=None):
        target = view if into is None else into
        batch = []
        for dsts, mask in transfers:
            ids = []
            for c in dsts:
                rid, pid, _ = topo.addr(c)
                ids.append(DstId(rid=rid, pnc=pid))
            batch.append(RemoteDMATransfer(dst_ids=ids, dma_engine_mask=mask, remote_sem=arrived,
                                           srcs=[view], dsts=[target for _ in dsts]))
            sent[0] += bits(mask)
        g.remote_dma_fused(batch, local_sem=sem.sent)

    def leg_to(j, is_a):
        for n, (s, transfers) in enumerate(legs(T, topo, j, is_a)):
            for dsts, mask in transfers:
                if core in dsts:
                    return n, bits(mask)

    def landed(j, is_a):
        return leg_to(j, is_a)[1]

    def spread(j, is_a):
        codes, plane = (T.qa[:], T.pa[:]) if is_a else (T.qv[:, cut(j, 128)], T.pv[:, cut(j, 128)])
        c_sem, s_sem = (sem.ca, sem.sa) if is_a else (sem["cv%d" % j], sem["sv%d" % j])
        for s, transfers in legs(T, topo, j, is_a):
            if s == core:
                if j != rank:
                    g.wait_ge(c_sem, landed(j, is_a))
                put(codes.bitcast(dt.uint8), transfers, c_sem)
                if j != rank:
                    g.wait_ge(s_sem, landed(j, is_a))
                put(plane, transfers, s_sem)

    w_queue = g.scalar
    if rank == root:
        w_queue = g.sync
        g.sync.dma_start(T.a_t[:], T.a[:]).then_inc(sem.ld_a, 16)
    g.sync.dma_start(T.bb_t[:], T.bb[:]).then_inc(sem.ld_b, 16)
    w_queue.dma_start(T.qw[:].bitcast(dt.uint8), T.wc[:]).then_inc(sem.ld_w, 16)
    w_queue.dma_start(T.pw[:], T.ws[:]).then_inc(sem.ld_w, 16)
    w_queue.dma_start(T.x_t[:], T.x[:]).then_inc(sem.ld_x, 16)

    here = [c for c in T.cores if topo.chip(c) == topo.chip(core)]
    place_here = here.index(core)
    before, after = here[place_here - 1], here[(place_here + 1) % len(here)]
    first, got = place_here, here.index(before)
    slots = [first, got] + [b for b in range(4) if b not in (first, got)]

    g.vector.memset(T.s_t[:, 0:512], 0.0).then_inc(sem.z1_ok, 1)
    g.vector.memset(T.s_t[:, 512:1536], 0.0).then_inc(sem.z2_ok, 1)
    ident = T.s_t[:, first:512:4]
    g.wait_ge(sem.z1_ok, 1)
    g.affine_select(ident, ident, [[-1, 128]], AluOpType.not_equal, 1.0, 0, 1).then_inc(sem.id_ok, 1)
    g.scalar.wait_ge(sem.z2_ok, 1)
    g.scalar.wait_ge(sem.id_ok, 1)
    for i in (1, 2):
        g.scalar.activation(T.s_t[:, 512 * i + slots[i + 1]:512 * i + 512:4], ident, copy).then_inc(sem.s_ok, 1)

    g.vector.wait_ge(sem.id_ok, 1)
    g.vector.quantize_mx(T.qs[:, 0:128], T.ps[:, 0:128], T.s_t[:, 0:512]).then_inc(sem.qs_ok, 1)
    if rank == root:
        g.vector.wait_ge(sem.ld_a, 16)
        g.vector.quantize_mx(T.qa[:], T.pa[:], T.a_t[:]).then_inc(sem.a_ok, 1)
    g.vector.wait_ge(sem.s_ok, 2)
    g.vector.quantize_mx(T.qs[:, 256:512], T.ps[:, 256:512], T.s_t[:, 512:1536]).then_inc(sem.qs_ok, 1)
    g.vector.wait_ge(sem.ld_b, 16)
    g.vector.quantize_mx(T.qb[:], T.pb[:], T.bb_t[:]).then_inc(sem.qb_ok, 1)
    g.vector.wait_ge(sem.ld_x, 16)
    g.vector.quantize_mx(T.qx[:], T.px[:], T.x_t[:]).then_inc(sem.qx_ok, 1)

    pass_on = [([after], topo.mask(core, after))]
    g.wait_ge(sem.qs_ok, 1)
    put(T.qs[:, 0:128].bitcast(dt.uint8), pass_on, sem.cs, T.qs[:, 128:256].bitcast(dt.uint8))
    put(T.ps[:, 0:128], pass_on, sem.ss, T.ps[:, 128:256])

    if rank == root:
        g.wait_ge(sem.a_ok, 1)
    spread(root, True)

    te = g.tensor
    te.wait_ge(sem.qs_ok, 2)
    te.wait_ge(sem.ld_w, 32)
    for i in (0, 2, 3, 1):
        if i == 1:
            te.wait_ge(sem.cs, bits(topo.mask(before, core)))
            te.wait_ge(sem.ss, bits(topo.mask(before, core)))
        te.matmul_mx(T.d[:, 512 * slots[i]:512 * slots[i] + 128], T.qs[:, cut(i, 128)], T.ps[:, cut(i, 128)],
                     T.qw[:], T.pw[:], True, True).then_inc(sem.d_ok, 1)
    te.wait_ge(sem.qb_ok, 1)
    if rank == root:
        te.wait_ge(sem.a_ok, 1)
    else:
        te.wait_ge(sem.ca, landed(root, True))
        te.wait_ge(sem.sa, landed(root, True))
    for b in range(4):
        te.matmul_mx(T.p[:, 512 * b:512 * b + 128], T.qb[:, cut(b, 128)], T.pb[:, cut(b, 128)],
                     T.qa[:], T.pa[:], True, True).then_inc(sem["prod%d" % b], 1)

    g.vector.wait_ge(sem.d_ok, 4)
    for b in range(4):
        scaled, product = T.m[:, cut(b, 128)], T.p[:, 512 * b:512 * b + 128]
        if b == 0:
            g.vector.wait_ge(sem["prod%d" % b], 1)
            g.vector.tensor_scalar(scaled, product, SCALE, None, AluOpType.mult).then_inc(sem["mul%d" % b], 1)
        else:
            g.scalar.wait_ge(sem["prod%d" % b], 1)
            g.scalar.activation(scaled, product, copy, scale=SCALE).then_inc(sem["mul%d" % b], 1)
        g.vector.wait_ge(sem["mul%d" % b], 1)
        g.vector.tensor_tensor(T.v_t[:, b:512:4], scaled, T.d[:, 512 * b:512 * b + 128],
                               AluOpType.add).then_inc(sem["add%d" % b], 1)
    for b in range(4):
        g.vector.wait_ge(sem["add%d" % b], 1)
    mine = cut(rank, 128)
    g.vector.quantize_mx(T.qv[:, mine], T.pv[:, mine], T.v_t[:]).then_inc(sem.v_ok, 1)

    g.wait_ge(sem.v_ok, 1)
    spread(rank, False)
    for j in range(N):
        if j != rank:
            spread(j, False)

    turns = {root: 0}
    for c in T.cores:
        for n, (s, transfers) in enumerate(legs(T, topo, root, True)):
            if any(c in dsts for dsts, mask in transfers):
                turns[T.rank_of(c)] = 1 if n == 0 else 2

    def place(j):
        return (j != rank, j != rank and turns[j] + 2 * leg_to(j, False)[0], j)

    te.wait_ge(sem.qx_ok, 1)
    te.wait_ge(sem.v_ok, 1)
    for k, j in enumerate(sorted(range(N), key=place)):
        bank = T.p[:, 512 * k:512 * k + 128] if k < 4 else T.d[:, 512 * (k - 4):512 * (k - 4) + 128]
        if j != rank:
            te.wait_ge(sem["cv%d" % j], landed(j, False))
            te.wait_ge(sem["sv%d" % j], landed(j, False))
        te.matmul_mx(bank, T.qv[:, cut(j, 128)], T.pv[:, cut(j, 128)], T.qx[:], T.px[:], True, True).then_inc(sem["y%d" % j], 1)
        out = T.yo[:, cut(j, NC)]
        if k % 2:
            g.vector.wait_ge(sem["y%d" % j], 1)
            g.vector.tensor_copy(out, bank).then_inc(sem["o%d" % j], 1)
        else:
            g.scalar.wait_ge(sem["y%d" % j], 1)
            g.scalar.activation(out, bank, copy).then_inc(sem["o%d" % j], 1)
        g.sync.wait_ge(sem["o%d" % j], 1)
        g.sync.dma_start(T.y[:, cut(j, NC)], out).then_inc(sem.st, 16)
    g.sync.wait_ge(sem.st, 16 * N)
    g.wait_ge(sem.sent, sent[0])
